import numpy as np
import ml_dtypes


def mxq(x, axis, fmt="e4m3"):
    dtype, down = {"e4m3": (ml_dtypes.float8_e4m3fn, 7), "e5m2": (ml_dtypes.float8_e5m2, 14)}[fmt]
    v = np.moveaxis(np.asarray(x, np.float32).astype(ml_dtypes.bfloat16).astype(np.float64), axis, -1)
    blocks = v.reshape(v.shape[:-1] + (-1, 32))
    amax = np.abs(blocks).max(-1, keepdims=True)
    byte = np.maximum(np.where(amax > 0, np.frexp(amax)[1] - 1 + 127, 0) - down, 1)
    scale = np.exp2(byte - 127.0)
    codes = (blocks / scale).astype(np.float32).astype(dtype).astype(np.float64)
    return np.moveaxis((codes * scale).reshape(v.shape), -1, axis)


WIDE = False


def mx_kscale(k):
    if not WIDE:
        return np.ones(k)
    levels = np.array([10, -10, 5, -5, 0])
    if k % 512:
        return np.exp2(np.random.permutation(np.resize(levels, k // 32))).repeat(32)
    a = np.empty((k // 512, 16))
    for p in range(k // 512):
        a[p, :8] = np.random.permutation(np.resize(levels, 8))
        for g in range(8):
            far = levels[np.abs(levels - a[p, g]) >= 10]
            a[p, g + 8] = far[np.random.randint(len(far))]
    return np.exp2(a.ravel()).repeat(32)


def f64(x):
    return np.asarray(x).astype(np.float64)


def striped(idx):
    return np.tile(idx.reshape(-1, 16).T, (8, 1)).astype(np.uint16)


def unstriped(offs):
    return offs[:16].T.reshape(-1).astype(np.int64)


E2M1 = np.array([0.0, 0.5, 1.0, 1.5, 2.0, 3.0, 4.0, 6.0, -0.0, -0.5, -1.0, -1.5, -2.0, -3.0, -4.0, -6.0])


def pack_weight(w, fmt):
    k, n = w.shape
    w = f64(np.asarray(w, np.float32).astype(ml_dtypes.bfloat16)).reshape(k // 32, 32, n)
    amax = np.abs(w).max(1)
    if fmt == "e4m3":
        byte = np.frexp(amax)[1] - 1 + 127 - 7
    else:
        mant, ex = np.frexp(amax / 6.0)
        byte = np.where(mant > 0.5, ex, ex - 1) + 127
    byte = np.clip(np.where(amax > 0, byte, 1), 1, 254)
    scaled = (w * np.exp2(127.0 - byte)[:, None, :]).reshape(k, n).astype(np.float32)
    by_word = np.ascontiguousarray(scaled.reshape(k // 512, 128, 4, n).transpose(0, 1, 3, 2))
    if fmt == "e4m3":
        words = by_word.astype(ml_dtypes.float8_e4m3fn).view(np.uint8)
    else:
        c = by_word.astype(ml_dtypes.float4_e2m1fn).view(np.uint8) & 0xF
        words = (c[..., 0::2] | (c[..., 1::2] << 4)).reshape(k // 512, 128, 2 * n)
    return np.ascontiguousarray(words), np.ascontiguousarray(byte.astype(np.uint8).reshape(k // 512, 16, n))


def unpack_weight(words, scales, fmt):
    g, _, n = scales.shape
    words = np.ascontiguousarray(words).reshape(g, 128, n, -1)
    if fmt == "e4m3":
        vals = words.view(ml_dtypes.float8_e4m3fn).astype(np.float64)
    else:
        nib = np.empty((g, 128, n, 4), np.uint8)
        nib[..., 0::2] = words & 0xF
        nib[..., 1::2] = words >> 4
        vals = E2M1[nib]
    vals = vals * np.repeat(np.exp2(scales.astype(np.float64) - 127.0), 8, axis=1)[..., None]
    return vals.transpose(0, 1, 3, 2).reshape(g * 512, n)


def gelu(v):
    return 0.5 * v * (1.0 + np.tanh(np.sqrt(2.0 / np.pi) * (v + 0.044715 * v**3)))


K, T, S, H, T3, S2, P = 1536, 4096, 1024, 512, 2048, 1024, 512

def setup_inputs():
    n = np.random.standard_normal
    s = mx_kscale(K)[:, None]
    u = mx_kscale(H)[:, None]
    d = {}
    d["tab_words"], d["tab_scales"] = pack_weight(n((K, T)) * s, "e4m3")
    d["offs"] = striped(np.random.permutation(T)[:S])
    d["w1"] = (1.5 * n((K, H)) / K ** 0.5 / s).astype(np.float32)
    d["w4_words"], d["w4_scales"] = pack_weight(1.2 * n((K, H)) / K ** 0.5 / s, "e2m1")
    d["cap"] = (0.5 * n(S)).astype(np.float32)
    d["gain"] = (np.exp(0.3 * n(H)) * u[:, 0]).astype(np.float32)
    d["tab2_words"], d["tab2_scales"] = pack_weight(n((H, T3)) / H ** 0.5 / u, "e4m3")
    d["offs2"] = striped(np.random.permutation(T3)[:S2])
    d["danger"] = np.exp(0.3 * n(S2)).astype(np.float32)
    d["pos1"] = striped(np.random.permutation(S)[:P])
    d["pos2"] = striped(np.random.permutation(S)[:P])
    return d

def reference(tab_words, tab_scales, offs, w1, w4_words, w4_scales, cap, gain,
              tab2_words, tab2_scales, offs2, danger, pos1, pos2):
    v = unpack_weight(tab_words, tab_scales, "e4m3")[:, unstriped(offs)]
    v2 = unpack_weight(tab2_words, tab2_scales, "e4m3")[:, unstriped(offs2)]
    w4 = unpack_weight(w4_words, w4_scales, "e2m1")
    a = mxq(f64(w1), 0, "e4m3").T @ v
    b = w4.T @ v
    h = f64(gain)[:, None] * (np.minimum(a, f64(cap)[None, :]) - b)
    hq = mxq(h, 0, "e4m3")
    e = v2.T @ hq
    e1 = e[:, unstriped(pos1)]
    e2 = e[:, unstriped(pos2)]
    f1 = 1.0 / (1.0 + np.exp(-e1))
    f2 = 1.0 / (1.0 + np.exp(-e2))
    return f64(danger)[:, None] * (f1 * f2)

@@ -1,0 +1,250 @@
+from contextlib import ExitStack
+
+import concourse.mybir as mybir
+from concourse.masks import make_identity
+
+K, T, S, H, T2, S2, NPAIR = 1536, 4096, 1024, 512, 2048, 1024, 512
+FLOPS = 2 * (2 * K * H * S) + 2 * H * S2 * S
+
+F32 = mybir.dt.float32
+BF16 = mybir.dt.bfloat16
+I32 = mybir.dt.int32
+U32 = mybir.dt.uint32
+U16 = mybir.dt.uint16
+U8 = mybir.dt.uint8
+FP8X4 = mybir.dt.float8_e4m3fn_x4
+FP4X4 = mybir.dt.float4_e2m1fn_x4
+ALU = mybir.AluOpType
+ACT = mybir.ActivationFunctionType
+
+P = 128
+PACK = 4
+PASSES = K // (P * PACK)
+QUADS = 4
+J_TILES = S // P
+M_TILES = S2 // P
+BANK = 512
+BANKS = 8
+
+
+def tile_list_swab_mode_scores_kernel(
+    tc, tab_words, tab_scales, offs, w1, w4_words, w4_scales, cap, gain,
+    tab2_words, tab2_scales, offs2, danger, pos1, pos2, out,
+):
+    nc = tc.nc
+    with ExitStack() as ctx:
+        keep = ctx.enter_context(tc.tile_pool(name="keep", bufs=1))
+        ring = ctx.enter_context(tc.tile_pool(name="ring", bufs=3))
+        psum = ctx.enter_context(tc.psum_pool(name="psum", bufs=1))
+
+        def bank(b, shape):
+            return psum.tile(shape, F32, name="bank%d" % b, tag="bank%d" % b)
+
+        def staged(slot, shape, dtype):
+            return keep.tile(shape, dtype, name="slot%d" % slot, tag="slot%d" % slot, align_bytes=64)
+
+        def words_of(table, a):
+            return table[a].rearrange("p n i -> p (n i)").bitcast(I32)
+
+        idx = keep.tile([P, S // 16], U16, name="idx")
+        idx2 = keep.tile([P, S2 // 16], U16, name="idx2")
+        p1 = keep.tile([P, NPAIR // 16], U16, name="p1")
+        p2 = keep.tile([P, NPAIR // 16], U16, name="p2")
+        nc.sync.dma_start(idx[:], offs)
+        nc.sync.dma_start(idx2[:], offs2)
+        nc.sync.dma_start(p1[:], pos1)
+        nc.sync.dma_start(p2[:], pos2)
+
+        ident = keep.tile([P, P], F32, name="ident")
+        cap_rows = staged(2, [P, P], F32)
+        nc.gpsimd.memset(cap_rows[:], 0.0)
+        make_identity(nc, ident[:])
+        nc.scalar.dma_start(cap_rows[0:J_TILES, :], cap.rearrange("(t p) -> t p", p=P))
+
+        def rows_to_columns(rows, via, name):
+            cols = keep.tile([P, J_TILES], F32, name=name)
+            nc.tensor.transpose(via[:, 0:P], rows[:], ident[:])
+            nc.scalar.copy(cols[:], via[:, 0:J_TILES])
+            return cols
+
+        cap_cols = rows_to_columns(cap_rows, bank(BANKS - 1, [P, P]), "cap_cols")
+
+        tab_scale_rows = staged(1, [P, T], U8)
+        nc.vector.memset(tab_scale_rows[:].bitcast(I32), 0)
+        w4_scale = keep.tile([P, PASSES, H], U8, name="w4_scale", align_bytes=64)
+        nc.vector.memset(w4_scale[:].rearrange("p a r -> p (a r)").bitcast(I32), 0)
+        tab2_scale_rows = keep.tile([P, T2], U8, name="tab2_scale_rows")
+        nc.vector.memset(tab2_scale_rows[:].bitcast(I32), 0)
+        v_scale = keep.tile([P, PASSES, S], U8, name="v_scale", align_bytes=64)
+        nc.vector.memset(v_scale[:].rearrange("p a j -> p (a j)").bitcast(I32), 0)
+
+        def load_words(slot, table, a, width):
+            tile = staged(slot, [P, width], U32)
+            nc.sync.dma_start(tile[:].bitcast(I32), words_of(table, a))
+            return tile
+
+        tab_tiles = [load_words(0, tab_words, 0, T)]
+        w4_codes = keep.tile([P, PASSES, 2 * H], U8, name="w4_codes", align_bytes=64)
+        nc.sync.dma_start(w4_codes[:].bitcast(I32), w4_words.rearrange("a p c -> p a c").bitcast(I32))
+        nc.scalar.dma_start(
+            tab_scale_rows[0 : 16 * PASSES, :].bitcast(I32),
+            tab_scales.rearrange("a q t -> q a t").bitcast(I32),
+        )
+        for q in range(QUADS):
+            nc.scalar.dma_start(
+                w4_scale[32 * q : 32 * q + 4, :, :].bitcast(I32),
+                w4_scales[:, 4 * q : 4 * q + 4, :].rearrange("a q r -> q a r").bitcast(I32),
+            )
+        for q in range(QUADS):
+            nc.gpsimd.dma_start(
+                tab2_scale_rows[32 * q : 32 * q + 4, :].bitcast(I32),
+                tab2_scales[0, 4 * q : 4 * q + 4, :].bitcast(I32),
+            )
+        tab_tiles.append(load_words(2, tab_words, 1, T))
+        danger_rows = keep.tile([P, P], F32, name="danger_rows")
+        nc.gpsimd.memset(danger_rows[:], 0.0)
+        nc.gpsimd.dma_start(danger_rows[0:M_TILES, :], danger.rearrange("(t p) -> t p", p=P))
+        gain_sb = keep.tile([P, PACK], F32, name="gain_sb")
+        nc.gpsimd.dma_start(gain_sb[:], gain.rearrange("(p i) -> p i", i=PACK))
+
+        picked_scale_rows = staged(4, [P, S], U8)
+        nc.vector.tensor_copy(picked_scale_rows[:], tab_scale_rows[:].indirect(idx[:]))
+        for q in range(QUADS):
+            nc.scalar.dma_start(
+                v_scale[32 * q : 32 * q + 4, :, :].bitcast(I32),
+                picked_scale_rows[12 * q : 12 * q + 12, :].bitcast(I32),
+            )
+
+        v_codes = [staged(1, [P, S], U32)] + [
+            keep.tile([P, S], U32, name="v_codes%d" % a, align_bytes=64) for a in range(1, PASSES)
+        ]
+        v2_scale = keep.tile([P, S2], U8, name="v2_scale", align_bytes=64)
+        b_banks = [bank(jt, [P, BANK]) for jt in range(J_TILES)]
+
+        def gather_words(dst, table, offsets, lo, hi):
+            nc.vector.tensor_copy(dst[:, lo:hi], table[:].indirect(offsets[:, lo // 16 : hi // 16]))
+
+        def first_product(acc, jt, a, codes, scale):
+            cols = slice(jt * P, (jt + 1) * P)
+            nc.tensor.matmul_mx(
+                out=acc[:], lhsT=v_codes[a][:, cols].bitcast(FP8X4), lhsT_scale=v_scale[:, a, cols],
+                rhs=codes, rhs_scale=scale, start=(a == 0), stop=(a == PASSES - 1),
+            )
+
+        def load_w1(a, raw):
+            nc.sync.dma_start(raw, w1[a * P * PACK : (a + 1) * P * PACK, :].rearrange("(p i) r -> p i r", i=PACK))
+            return raw
+
+        gather_words(v_codes[0], tab_tiles[0], idx, 0, S)
+        tab_tiles.append(load_words(0, tab_words, 2, T))
+        w1_raw = [load_w1(0, staged(4, [P, PACK, H], F32)[:])]
+        gather_words(v_codes[1], tab_tiles[1], idx, 0, S)
+        w1_late = staged(2, [P, PASSES - 1, PACK, H], F32)
+        w1_raw.extend(load_w1(a, w1_late[:, a - 1, :, :]) for a in range(1, PASSES))
+        nc.vector.tensor_copy(v2_scale[:], tab2_scale_rows[:].indirect(idx2[:]))
+        gather_words(v_codes[2], tab_tiles[2], idx, 0, S // 2)
+        gather_words(v_codes[2], tab_tiles[2], idx, S // 2, S)
+        tab2_tile = load_words(0, tab2_words, 0, T2)
+
+        for a in range(PASSES):
+            for jt in range(J_TILES):
+                first_product(b_banks[jt], jt, a, w4_codes[:, a, :].bitcast(FP4X4), w4_scale[:, a, :])
+        b_sb = keep.tile([P, J_TILES, PACK, P], F32, name="b_sb")
+        for jt in range(J_TILES):
+            nc.scalar.copy(b_sb[:, jt, :, :], b_banks[jt][:].rearrange("j (p i) -> j i p", i=PACK))
+        danger_cols = rows_to_columns(danger_rows, b_banks[J_TILES - 1], "danger_cols")
+
+        w1_codes = keep.tile([P, PASSES, H], U32, name="w1_codes", align_bytes=64)
+        w1_scale = keep.tile([P, PASSES, H], U8, name="w1_scale", align_bytes=64)
+        for a in range(PASSES):
+            w1_bf = ring.tile([P, H, PACK], BF16, name="w1_bf", align_bytes=64)
+            nc.vector.tensor_copy(
+                w1_bf[:].rearrange("p (c n) i -> p c i n", n=4),
+                w1_raw[a].rearrange("p i (c n) -> p c i n", n=4),
+            )
+            nc.vector.quantize_mx(
+                out=w1_codes[:, a, :].bitcast(FP8X4), scales=w1_scale[:, a, :],
+                in_=w1_bf[:].rearrange("p r i -> p (r i)"),
+            )
+
+        A_BANKS = 6
+        a_banks = {}
+
+        def response(jt, passes):
+            if jt not in a_banks:
+                a_banks[jt] = bank(jt % A_BANKS, [P, BANK])
+            for a in passes:
+                first_product(a_banks[jt], jt, a, w1_codes[:, a, :].bitcast(FP8X4), w1_scale[:, a, :])
+
+        for a in range(PASSES - 1):
+            for jt in range(A_BANKS):
+                response(jt, [a])
+
+        h_bf = keep.tile([P, S, PACK], BF16, name="h_bf", align_bytes=64)
+        h_codes = keep.tile([P, S], U32, name="h_codes", align_bytes=64)
+        h_scale = keep.tile([P, S], U8, name="h_scale", align_bytes=64)
+        v2_codes = keep.tile([P, S2], U32, name="v2_codes", align_bytes=64)
+        u_banks = {}
+
+        def capped(jt):
+            u = ring.tile([P, PACK, P], F32, name="u")
+            nc.vector.scalar_tensor_tensor(
+                out=u[:], in0=a_banks[jt][:].rearrange("j (p i) -> j i p", i=PACK),
+                scalar=cap_cols[:, jt : jt + 1], in1=b_sb[:, jt, :, :],
+                op0=ALU.min, op1=ALU.subtract,
+            )
+            u_banks[jt] = bank(A_BANKS + jt % 2, [P, PACK, P])
+            for i in range(PACK):
+                nc.tensor.transpose(u_banks[jt][:, i, :], u[:, i, :], ident[:])
+
+        def gained(jt):
+            nc.vector.tensor_tensor(
+                out=h_bf[:, jt * P : (jt + 1) * P, :],
+                in0=u_banks[jt][:].rearrange("p i j -> p j i"),
+                in1=gain_sb[:].unsqueeze(1).to_broadcast([P, P, PACK]),
+                op=ALU.mult,
+            )
+
+        def quantize_h(lo, hi):
+            nc.vector.quantize_mx(
+                out=h_codes[:, lo:hi].bitcast(FP8X4), scales=h_scale[:, lo:hi],
+                in_=h_bf[:, lo:hi, :].rearrange("p j i -> p (j i)"),
+            )
+
+        for jt in range(A_BANKS):
+            response(jt, [PASSES - 1])
+        for jt in range(J_TILES + 1):
+            if jt < J_TILES:
+                capped(jt)
+            if jt + A_BANKS < J_TILES:
+                response(jt + A_BANKS, range(PASSES))
+            if jt >= 1:
+                gained(jt - 1)
+            if jt == 5:
+                quantize_h(0, S // 2)
+        gather_words(v2_codes, tab2_tile, idx2, 0, 256)
+        quantize_h(S // 2, S)
+        gather_words(v2_codes, tab2_tile, idx2, 256, S2)
+
+        for mt in range(M_TILES):
+            rows = slice(mt * P, (mt + 1) * P)
+            e_sb = ring.tile([P, S], F32, name="e_sb")
+            for half in range(2):
+                cols = slice(half * BANK, (half + 1) * BANK)
+                e_bank = bank(2 + (2 * mt + half) % 4, [P, BANK])
+                nc.tensor.matmul_mx(
+                    out=e_bank[:], lhsT=v2_codes[:, rows].bitcast(FP8X4), lhsT_scale=v2_scale[:, rows],
+                    rhs=h_codes[:, cols].bitcast(FP8X4), rhs_scale=h_scale[:, cols], start=True, stop=True,
+                )
+                nc.scalar.copy(e_sb[:, cols], e_bank[:])
+            picked = ring.tile([P, 2, NPAIR], F32, name="picked")
+            sig = ring.tile([P, 2, NPAIR], F32, name="sig")
+            for mode, pos in enumerate((p1, p2)):
+                nc.vector.tensor_copy(picked[:, mode, :], e_sb[:].indirect(pos[:]))
+                nc.scalar.activation(sig[:, mode, :], picked[:, mode, :], ACT.Sigmoid)
+            res = ring.tile([P, NPAIR], F32, name="res")
+            nc.vector.scalar_tensor_tensor(
+                out=res[:], in0=sig[:, 0, :], scalar=danger_cols[:, mt : mt + 1],
+                in1=sig[:, 1, :], op0=ALU.mult, op1=ALU.mult,
+            )
+            nc.sync.dma_start(out[rows, :], res[:])

@@ -55,21 +55,7 @@ def tile_list_swab_mode_scores_kernel(
         nc.sync.dma_start(p1[:], pos1)
         nc.sync.dma_start(p2[:], pos2)
 
-        ident = keep.tile([P, P], F32, name="ident")
-        cap_rows = staged(2, [P, P], F32)
-        nc.gpsimd.memset(cap_rows[:], 0.0)
-        make_identity(nc, ident[:])
-        nc.scalar.dma_start(cap_rows[0:J_TILES, :], cap.rearrange("(t p) -> t p", p=P))
-
-        def rows_to_columns(rows, via, name):
-            cols = keep.tile([P, J_TILES], F32, name=name)
-            nc.tensor.transpose(via[:, 0:P], rows[:], ident[:])
-            nc.scalar.copy(cols[:], via[:, 0:J_TILES])
-            return cols
-
-        cap_cols = rows_to_columns(cap_rows, bank(BANKS - 1, [P, P]), "cap_cols")
-
-        tab_scale_rows = staged(1, [P, T], U8)
+        tab_scale_rows = keep.tile([P, T], U8, name="tab_scale_rows")
         nc.vector.memset(tab_scale_rows[:].bitcast(I32), 0)
         w4_scale = keep.tile([P, PASSES, H], U8, name="w4_scale", align_bytes=64)
         nc.vector.memset(w4_scale[:].rearrange("p a r -> p (a r)").bitcast(I32), 0)
@@ -78,47 +64,71 @@ def tile_list_swab_mode_scores_kernel(
         v_scale = keep.tile([P, PASSES, S], U8, name="v_scale", align_bytes=64)
         nc.vector.memset(v_scale[:].rearrange("p a j -> p (a j)").bitcast(I32), 0)
 
-        def load_words(slot, table, a, width):
-            tile = staged(slot, [P, width], U32)
+        def load_words(tile, table, a):
             nc.sync.dma_start(tile[:].bitcast(I32), words_of(table, a))
             return tile
 
-        tab_tiles = [load_words(0, tab_words, 0, T)]
-        w4_codes = keep.tile([P, PASSES, 2 * H], U8, name="w4_codes", align_bytes=64)
-        nc.sync.dma_start(w4_codes[:].bitcast(I32), w4_words.rearrange("a p c -> p a c").bitcast(I32))
-        nc.scalar.dma_start(
+        def load_w1(a):
+            raw = keep.tile([P, PACK, H], F32, name="w1_raw%d" % a)
+            nc.sync.dma_start(raw[:], w1[a * P * PACK : (a + 1) * P * PACK, :].rearrange("(p i) r -> p i r", i=PACK))
+            return raw
+
+        w1_codes = keep.tile([P, PASSES, H], U32, name="w1_codes", align_bytes=64)
+        w1_scale = keep.tile([P, PASSES, H], U8, name="w1_scale", align_bytes=64)
+
+        def quantize_w1(a):
+            w1_bf = ring.tile([P, H, PACK], BF16, name="w1_bf", align_bytes=64)
+            nc.vector.tensor_copy(
+                w1_bf[:].rearrange("p (c n) i -> p c i n", n=4),
+                w1_raw[a][:].rearrange("p i (c n) -> p c i n", n=4),
+            )
+            nc.vector.quantize_mx(
+                out=w1_codes[:, a, :].bitcast(FP8X4), scales=w1_scale[:, a, :],
+                in_=w1_bf[:].rearrange("p r i -> p (r i)"),
+            )
+
+        w1_raw = [load_w1(0)]
+        nc.sync.dma_start(
             tab_scale_rows[0 : 16 * PASSES, :].bitcast(I32),
             tab_scales.rearrange("a q t -> q a t").bitcast(I32),
         )
+        w4_codes = keep.tile([P, PASSES, 2 * H], U8, name="w4_codes", align_bytes=64)
+        nc.sync.dma_start(w4_codes[:].bitcast(I32), w4_words.rearrange("a p c -> p a c").bitcast(I32))
+        tab_tiles = [load_words(keep.tile([P, T], U32, name="tab_first"), tab_words, 0)]
         for q in range(QUADS):
-            nc.scalar.dma_start(
+            nc.sync.dma_start(
                 w4_scale[32 * q : 32 * q + 4, :, :].bitcast(I32),
                 w4_scales[:, 4 * q : 4 * q + 4, :].rearrange("a q r -> q a r").bitcast(I32),
             )
+        tab_tiles.append(load_words(staged(0, [P, T], U32), tab_words, 1))
+        quantize_w1(0)
+
+        picked_scale_rows = keep.tile([P, S], U8, name="picked_scale_rows")
+        nc.vector.tensor_copy(picked_scale_rows[:], tab_scale_rows[:].indirect(idx[:]))
+        for q in range(QUADS):
+            nc.sync.dma_start(
+                v_scale[32 * q : 32 * q + 4, :, :].bitcast(I32),
+                picked_scale_rows[12 * q : 12 * q + 12, :].bitcast(I32),
+            )
+        tab_tiles.append(load_words(keep.tile([P, T], U32, name="tab_last"), tab_words, 2))
+        w1_raw.extend(load_w1(a) for a in range(1, PASSES))
+        tab2_tile = load_words(keep.tile([P, T2], U32, name="tab2_tile"), tab2_words, 0)
+
         for q in range(QUADS):
             nc.gpsimd.dma_start(
                 tab2_scale_rows[32 * q : 32 * q + 4, :].bitcast(I32),
                 tab2_scales[0, 4 * q : 4 * q + 4, :].bitcast(I32),
             )
-        tab_tiles.append(load_words(2, tab_words, 1, T))
-        danger_rows = keep.tile([P, P], F32, name="danger_rows")
-        nc.gpsimd.memset(danger_rows[:], 0.0)
-        nc.gpsimd.dma_start(danger_rows[0:M_TILES, :], danger.rearrange("(t p) -> t p", p=P))
+        ident = keep.tile([P, P], F32, name="ident")
+        make_identity(nc, ident[:])
+        vec_rows = keep.tile([P, P], F32, name="vec_rows")
+        nc.gpsimd.memset(vec_rows[:], 0.0)
+        for n, vec in enumerate((cap, danger)):
+            nc.gpsimd.dma_start(vec_rows[n * J_TILES : (n + 1) * J_TILES, :], vec.rearrange("(t p) -> t p", p=P))
         gain_sb = keep.tile([P, PACK], F32, name="gain_sb")
         nc.gpsimd.dma_start(gain_sb[:], gain.rearrange("(p i) -> p i", i=PACK))
 
-        picked_scale_rows = staged(4, [P, S], U8)
-        nc.vector.tensor_copy(picked_scale_rows[:], tab_scale_rows[:].indirect(idx[:]))
-        for q in range(QUADS):
-            nc.scalar.dma_start(
-                v_scale[32 * q : 32 * q + 4, :, :].bitcast(I32),
-                picked_scale_rows[12 * q : 12 * q + 12, :].bitcast(I32),
-            )
-
-        v_codes = [staged(1, [P, S], U32)] + [
-            keep.tile([P, S], U32, name="v_codes%d" % a, align_bytes=64) for a in range(1, PASSES)
-        ]
-        v2_scale = keep.tile([P, S2], U8, name="v2_scale", align_bytes=64)
+        v_codes = [keep.tile([P, S], U32, name="v_codes%d" % a, align_bytes=64) for a in range(PASSES)]
         b_banks = [bank(jt, [P, BANK]) for jt in range(J_TILES)]
 
         def gather_words(dst, table, offsets, lo, hi):
@@ -131,20 +141,12 @@ def tile_list_swab_mode_scores_kernel(
                 rhs=codes, rhs_scale=scale, start=(a == 0), stop=(a == PASSES - 1),
             )
 
-        def load_w1(a, raw):
-            nc.sync.dma_start(raw, w1[a * P * PACK : (a + 1) * P * PACK, :].rearrange("(p i) r -> p i r", i=PACK))
-            return raw
-
         gather_words(v_codes[0], tab_tiles[0], idx, 0, S)
-        tab_tiles.append(load_words(0, tab_words, 2, T))
-        w1_raw = [load_w1(0, staged(4, [P, PACK, H], F32)[:])]
         gather_words(v_codes[1], tab_tiles[1], idx, 0, S)
-        w1_late = staged(2, [P, PASSES - 1, PACK, H], F32)
-        w1_raw.extend(load_w1(a, w1_late[:, a - 1, :, :]) for a in range(1, PASSES))
+        v2_scale = staged(0, [P, S2], U8)
         nc.vector.tensor_copy(v2_scale[:], tab2_scale_rows[:].indirect(idx2[:]))
         gather_words(v_codes[2], tab_tiles[2], idx, 0, S // 2)
         gather_words(v_codes[2], tab_tiles[2], idx, S // 2, S)
-        tab2_tile = load_words(0, tab2_words, 0, T2)
 
         for a in range(PASSES):
             for jt in range(J_TILES):
@@ -152,20 +154,13 @@ def tile_list_swab_mode_scores_kernel(
         b_sb = keep.tile([P, J_TILES, PACK, P], F32, name="b_sb")
         for jt in range(J_TILES):
             nc.scalar.copy(b_sb[:, jt, :, :], b_banks[jt][:].rearrange("j (p i) -> j i p", i=PACK))
-        danger_cols = rows_to_columns(danger_rows, b_banks[J_TILES - 1], "danger_cols")
+        vec_bank = b_banks[J_TILES - 1]
+        nc.tensor.transpose(vec_bank[:, 0:P], vec_rows[:], ident[:])
+        vec_cols = keep.tile([P, 2, J_TILES], F32, name="vec_cols")
+        nc.scalar.copy(vec_cols[:].rearrange("p n t -> p (n t)"), vec_bank[:, 0 : 2 * J_TILES])
 
-        w1_codes = keep.tile([P, PASSES, H], U32, name="w1_codes", align_bytes=64)
-        w1_scale = keep.tile([P, PASSES, H], U8, name="w1_scale", align_bytes=64)
-        for a in range(PASSES):
-            w1_bf = ring.tile([P, H, PACK], BF16, name="w1_bf", align_bytes=64)
-            nc.vector.tensor_copy(
-                w1_bf[:].rearrange("p (c n) i -> p c i n", n=4),
-                w1_raw[a].rearrange("p i (c n) -> p c i n", n=4),
-            )
-            nc.vector.quantize_mx(
-                out=w1_codes[:, a, :].bitcast(FP8X4), scales=w1_scale[:, a, :],
-                in_=w1_bf[:].rearrange("p r i -> p (r i)"),
-            )
+        for a in range(1, PASSES):
+            quantize_w1(a)
 
         A_BANKS = 6
         a_banks = {}
@@ -175,10 +170,6 @@ def tile_list_swab_mode_scores_kernel(
                 a_banks[jt] = bank(jt % A_BANKS, [P, BANK])
             for a in passes:
                 first_product(a_banks[jt], jt, a, w1_codes[:, a, :].bitcast(FP8X4), w1_scale[:, a, :])
-
-        for a in range(PASSES - 1):
-            for jt in range(A_BANKS):
-                response(jt, [a])
 
         h_bf = keep.tile([P, S, PACK], BF16, name="h_bf", align_bytes=64)
         h_codes = keep.tile([P, S], U32, name="h_codes", align_bytes=64)
@@ -190,7 +181,7 @@ def tile_list_swab_mode_scores_kernel(
             u = ring.tile([P, PACK, P], F32, name="u")
             nc.vector.scalar_tensor_tensor(
                 out=u[:], in0=a_banks[jt][:].rearrange("j (p i) -> j i p", i=PACK),
-                scalar=cap_cols[:, jt : jt + 1], in1=b_sb[:, jt, :, :],
+                scalar=vec_cols[:, 0, jt : jt + 1], in1=b_sb[:, jt, :, :],
                 op0=ALU.min, op1=ALU.subtract,
             )
             u_banks[jt] = bank(A_BANKS + jt % 2, [P, PACK, P])
@@ -212,7 +203,7 @@ def tile_list_swab_mode_scores_kernel(
             )
 
         for jt in range(A_BANKS):
-            response(jt, [PASSES - 1])
+            response(jt, range(PASSES))
         for jt in range(J_TILES + 1):
             if jt < J_TILES:
                 capped(jt)
@@ -239,12 +230,17 @@ def tile_list_swab_mode_scores_kernel(
                 nc.scalar.copy(e_sb[:, cols], e_bank[:])
             picked = ring.tile([P, 2, NPAIR], F32, name="picked")
             sig = ring.tile([P, 2, NPAIR], F32, name="sig")
-            for mode, pos in enumerate((p1, p2)):
-                nc.vector.tensor_copy(picked[:, mode, :], e_sb[:].indirect(pos[:]))
-                nc.scalar.activation(sig[:, mode, :], picked[:, mode, :], ACT.Sigmoid)
             res = ring.tile([P, NPAIR], F32, name="res")
-            nc.vector.scalar_tensor_tensor(
-                out=res[:], in0=sig[:, 0, :], scalar=danger_cols[:, mt : mt + 1],
-                in1=sig[:, 1, :], op0=ALU.mult, op1=ALU.mult,
-            )
-            nc.sync.dma_start(out[rows, :], res[:])
+            width = NPAIR // 2 if mt == M_TILES - 1 else NPAIR
+            for lo in range(0, NPAIR, width):
+                pairs = slice(lo, lo + width)
+                for mode, pos in enumerate((p1, p2)):
+                    nc.vector.tensor_copy(
+                        picked[:, mode, pairs], e_sb[:].indirect(pos[:, lo // 16 : (lo + width) // 16])
+                    )
+                    nc.scalar.activation(sig[:, mode, pairs], picked[:, mode, pairs], ACT.Sigmoid)
+                nc.vector.scalar_tensor_tensor(
+                    out=res[:, pairs], in0=sig[:, 0, pairs], scalar=vec_cols[:, 1, mt : mt + 1],
+                    in1=sig[:, 1, pairs], op0=ALU.mult, op1=ALU.mult,
+                )
+                nc.sync.dma_start(out[rows, pairs], res[:, pairs])

@@ -125,6 +125,10 @@ def tile_list_swab_mode_scores_kernel(
         nc.gpsimd.memset(vec_rows[:], 0.0)
         for n, vec in enumerate((cap, danger)):
             nc.gpsimd.dma_start(vec_rows[n * J_TILES : (n + 1) * J_TILES, :], vec.rearrange("(t p) -> t p", p=P))
+        vec_bank = bank(BANKS - 1, [P, P])
+        nc.tensor.transpose(vec_bank[:], vec_rows[:], ident[:])
+        vec_cols = keep.tile([P, 2, J_TILES], F32, name="vec_cols")
+        nc.scalar.copy(vec_cols[:].rearrange("p n t -> p (n t)"), vec_bank[:, 0 : 2 * J_TILES])
         gain_sb = keep.tile([P, PACK], F32, name="gain_sb")
         nc.gpsimd.dma_start(gain_sb[:], gain.rearrange("(p i) -> p i", i=PACK))
 
@@ -154,15 +158,11 @@ def tile_list_swab_mode_scores_kernel(
         b_sb = keep.tile([P, J_TILES, PACK, P], F32, name="b_sb")
         for jt in range(J_TILES):
             nc.scalar.copy(b_sb[:, jt, :, :], b_banks[jt][:].rearrange("j (p i) -> j i p", i=PACK))
-        vec_bank = b_banks[J_TILES - 1]
-        nc.tensor.transpose(vec_bank[:, 0:P], vec_rows[:], ident[:])
-        vec_cols = keep.tile([P, 2, J_TILES], F32, name="vec_cols")
-        nc.scalar.copy(vec_cols[:].rearrange("p n t -> p (n t)"), vec_bank[:, 0 : 2 * J_TILES])
 
         for a in range(1, PASSES):
             quantize_w1(a)
 
-        A_BANKS = 6
+        A_BANKS = 5
         a_banks = {}
 
         def response(jt, passes):
@@ -184,19 +184,24 @@ def tile_list_swab_mode_scores_kernel(
                 scalar=vec_cols[:, 0, jt : jt + 1], in1=b_sb[:, jt, :, :],
                 op0=ALU.min, op1=ALU.subtract,
             )
-            u_banks[jt] = bank(A_BANKS + jt % 2, [P, PACK, P])
+            u_banks[jt] = bank(A_BANKS + jt % (BANKS - A_BANKS), [P, PACK, P])
             for i in range(PACK):
                 nc.tensor.transpose(u_banks[jt][:, i, :], u[:, i, :], ident[:])
 
+        h_planes = keep.tile([P, PACK, S], BF16, name="h_planes")
+
         def gained(jt):
-            nc.vector.tensor_tensor(
-                out=h_bf[:, jt * P : (jt + 1) * P, :],
-                in0=u_banks[jt][:].rearrange("p i j -> p j i"),
-                in1=gain_sb[:].unsqueeze(1).to_broadcast([P, P, PACK]),
-                op=ALU.mult,
-            )
+            for i in range(PACK):
+                nc.scalar.activation(
+                    h_planes[:, i, jt * P : (jt + 1) * P], u_banks[jt][:, i, :], ACT.Copy,
+                    scale=gain_sb[:, i : i + 1],
+                )
 
         def quantize_h(lo, hi):
+            nc.vector.tensor_copy(
+                h_bf[:, lo:hi, :].rearrange("p (c n) i -> p c i n", n=4),
+                h_planes[:, :, lo:hi].rearrange("p i (c n) -> p c i n", n=4),
+            )
             nc.vector.quantize_mx(
                 out=h_codes[:, lo:hi].bitcast(FP8X4), scales=h_scale[:, lo:hi],
                 in_=h_bf[:, lo:hi, :].rearrange("p j i -> p (j i)"),
@@ -204,17 +209,15 @@ def tile_list_swab_mode_scores_kernel(
 
         for jt in range(A_BANKS):
             response(jt, range(PASSES))
-        for jt in range(J_TILES + 1):
-            if jt < J_TILES:
-                capped(jt)
+        for jt in range(J_TILES):
+            capped(jt)
             if jt + A_BANKS < J_TILES:
                 response(jt + A_BANKS, range(PASSES))
-            if jt >= 1:
-                gained(jt - 1)
-            if jt == 5:
-                quantize_h(0, S // 2)
+            gained(jt)
+            if jt >= 3 and jt % 2 == 1:
+                quantize_h((jt - 3) * P, (jt - 1) * P)
         gather_words(v2_codes, tab2_tile, idx2, 0, 256)
-        quantize_h(S // 2, S)
+        quantize_h(S - 2 * P, S)
         gather_words(v2_codes, tab2_tile, idx2, 256, S2)
 
         for mt in range(M_TILES):
@@ -222,7 +225,7 @@ def tile_list_swab_mode_scores_kernel(
             e_sb = ring.tile([P, S], F32, name="e_sb")
             for half in range(2):
                 cols = slice(half * BANK, (half + 1) * BANK)
-                e_bank = bank(2 + (2 * mt + half) % 4, [P, BANK])
+                e_bank = bank((3 + (2 * mt + half) % 4) % A_BANKS, [P, BANK])
                 nc.tensor.matmul_mx(
                     out=e_bank[:], lhsT=v2_codes[:, rows].bitcast(FP8X4), lhsT_scale=v2_scale[:, rows],
                     rhs=h_codes[:, cols].bitcast(FP8X4), rhs_scale=h_scale[:, cols], start=True, stop=True,

@@ -20,11 +20,18 @@ ACT = mybir.ActivationFunctionType
 P = 128
 PACK = 4
 PASSES = K // (P * PACK)
+BLOCKS = 16
 QUADS = 4
+ROWS = BLOCKS // QUADS
+STRIPE = 16
 J_TILES = S // P
 M_TILES = S2 // P
 BANK = 512
 BANKS = 8
+RESPONSE_BANKS = 5
+SCORE_BANKS = (3, 4, 0, 1)
+VECTOR_GAIN_TILES = 2
+FIRST_COMPOUNDS = 2 * P
 
 
 def tile_list_swab_mode_scores_kernel(
@@ -40,85 +47,91 @@ def tile_list_swab_mode_scores_kernel(
         def bank(b, shape):
             return psum.tile(shape, F32, name="bank%d" % b, tag="bank%d" % b)
 
-        def staged(slot, shape, dtype):
-            return keep.tile(shape, dtype, name="slot%d" % slot, tag="slot%d" % slot, align_bytes=64)
+        def zeroed(name, shape):
+            tile = keep.tile(shape, U8, name=name, align_bytes=64)
+            flat = tile[:] if len(shape) == 2 else tile[:].rearrange("p a c -> p (a c)")
+            nc.vector.memset(flat.bitcast(I32), 0)
+            return tile
 
-        def words_of(table, a):
-            return table[a].rearrange("p n i -> p (n i)").bitcast(I32)
+        def load_words(name, table, a):
+            tile = keep.tile([P, table.shape[2]], U32, name=name)
+            nc.sync.dma_start(tile[:].bitcast(I32), table[a].rearrange("p n i -> p (n i)").bitcast(I32))
+            return tile
 
-        idx = keep.tile([P, S // 16], U16, name="idx")
-        idx2 = keep.tile([P, S2 // 16], U16, name="idx2")
-        p1 = keep.tile([P, NPAIR // 16], U16, name="p1")
-        p2 = keep.tile([P, NPAIR // 16], U16, name="p2")
+        def load_w1(a):
+            raw = keep.tile([P, PACK, H], F32, name="w1_raw%d" % a)
+            rows = w1[a * P * PACK : (a + 1) * P * PACK, :]
+            nc.sync.dma_start(raw[:], rows.rearrange("(p i) r -> p i r", i=PACK))
+            return raw
+
+        def gather(dst, window, offsets, lo, hi):
+            nc.vector.tensor_copy(dst[:, lo:hi], window[:].indirect(offsets[:, lo // STRIPE : hi // STRIPE]))
+
+        def interleave(dst, src):
+            nc.vector.tensor_copy(
+                dst.rearrange("p (c n) i -> p c i n", n=4), src.rearrange("p i (c n) -> p c i n", n=4)
+            )
+
+        def quantize(codes, scale, grouped):
+            nc.vector.quantize_mx(
+                out=codes.bitcast(FP8X4), scales=scale, in_=grouped.rearrange("p c i -> p (c i)")
+            )
+
+        idx = keep.tile([P, S // STRIPE], U16, name="idx")
+        idx2 = keep.tile([P, S2 // STRIPE], U16, name="idx2")
+        p1 = keep.tile([P, NPAIR // STRIPE], U16, name="p1")
+        p2 = keep.tile([P, NPAIR // STRIPE], U16, name="p2")
         nc.sync.dma_start(idx[:], offs)
         nc.sync.dma_start(idx2[:], offs2)
         nc.sync.dma_start(p1[:], pos1)
         nc.sync.dma_start(p2[:], pos2)
 
-        tab_scale_rows = keep.tile([P, T], U8, name="tab_scale_rows")
-        nc.vector.memset(tab_scale_rows[:].bitcast(I32), 0)
-        w4_scale = keep.tile([P, PASSES, H], U8, name="w4_scale", align_bytes=64)
-        nc.vector.memset(w4_scale[:].rearrange("p a r -> p (a r)").bitcast(I32), 0)
-        tab2_scale_rows = keep.tile([P, T2], U8, name="tab2_scale_rows")
-        nc.vector.memset(tab2_scale_rows[:].bitcast(I32), 0)
-        v_scale = keep.tile([P, PASSES, S], U8, name="v_scale", align_bytes=64)
-        nc.vector.memset(v_scale[:].rearrange("p a j -> p (a j)").bitcast(I32), 0)
+        tab_scale_rows = zeroed("tab_scale_rows", [P, T])
+        tab2_scale_rows = zeroed("tab2_scale_rows", [P, T2])
+        w4_scale = zeroed("w4_scale", [P, PASSES, H])
+        v_scale = zeroed("v_scale", [P, PASSES, S])
 
-        def load_words(tile, table, a):
-            nc.sync.dma_start(tile[:].bitcast(I32), words_of(table, a))
-            return tile
-
-        def load_w1(a):
-            raw = keep.tile([P, PACK, H], F32, name="w1_raw%d" % a)
-            nc.sync.dma_start(raw[:], w1[a * P * PACK : (a + 1) * P * PACK, :].rearrange("(p i) r -> p i r", i=PACK))
-            return raw
+        w1_raw = [load_w1(0)]
+        nc.sync.dma_start(
+            tab_scale_rows[0 : BLOCKS * PASSES, :].bitcast(I32),
+            tab_scales.rearrange("a q t -> q a t").bitcast(I32),
+        )
+        w4_codes = keep.tile([P, PASSES, 2 * H], U8, name="w4_codes", align_bytes=64)
+        nc.sync.dma_start(w4_codes[:].bitcast(I32), w4_words.rearrange("a p c -> p a c").bitcast(I32))
+        for quad in range(QUADS):
+            nc.sync.dma_start(
+                tab2_scale_rows[32 * quad : 32 * quad + ROWS, :].bitcast(I32),
+                tab2_scales[0, ROWS * quad : ROWS * (quad + 1), :].bitcast(I32),
+            )
+        tab_tiles = [load_words("tab_first", tab_words, 0)]
+        for quad in range(QUADS):
+            nc.sync.dma_start(
+                w4_scale[32 * quad : 32 * quad + ROWS, :, :].bitcast(I32),
+                w4_scales[:, ROWS * quad : ROWS * (quad + 1), :].rearrange("a q r -> q a r").bitcast(I32),
+            )
+        tab_tiles.append(load_words("tab_mid", tab_words, 1))
 
         w1_codes = keep.tile([P, PASSES, H], U32, name="w1_codes", align_bytes=64)
         w1_scale = keep.tile([P, PASSES, H], U8, name="w1_scale", align_bytes=64)
 
         def quantize_w1(a):
             w1_bf = ring.tile([P, H, PACK], BF16, name="w1_bf", align_bytes=64)
-            nc.vector.tensor_copy(
-                w1_bf[:].rearrange("p (c n) i -> p c i n", n=4),
-                w1_raw[a][:].rearrange("p i (c n) -> p c i n", n=4),
-            )
-            nc.vector.quantize_mx(
-                out=w1_codes[:, a, :].bitcast(FP8X4), scales=w1_scale[:, a, :],
-                in_=w1_bf[:].rearrange("p r i -> p (r i)"),
-            )
+            interleave(w1_bf[:], w1_raw[a][:])
+            quantize(w1_codes[:, a, :], w1_scale[:, a, :], w1_bf[:])
 
-        w1_raw = [load_w1(0)]
-        nc.sync.dma_start(
-            tab_scale_rows[0 : 16 * PASSES, :].bitcast(I32),
-            tab_scales.rearrange("a q t -> q a t").bitcast(I32),
-        )
-        w4_codes = keep.tile([P, PASSES, 2 * H], U8, name="w4_codes", align_bytes=64)
-        nc.sync.dma_start(w4_codes[:].bitcast(I32), w4_words.rearrange("a p c -> p a c").bitcast(I32))
-        tab_tiles = [load_words(keep.tile([P, T], U32, name="tab_first"), tab_words, 0)]
-        for q in range(QUADS):
-            nc.sync.dma_start(
-                w4_scale[32 * q : 32 * q + 4, :, :].bitcast(I32),
-                w4_scales[:, 4 * q : 4 * q + 4, :].rearrange("a q r -> q a r").bitcast(I32),
-            )
-        tab_tiles.append(load_words(staged(0, [P, T], U32), tab_words, 1))
         quantize_w1(0)
 
         picked_scale_rows = keep.tile([P, S], U8, name="picked_scale_rows")
-        nc.vector.tensor_copy(picked_scale_rows[:], tab_scale_rows[:].indirect(idx[:]))
-        for q in range(QUADS):
+        gather(picked_scale_rows, tab_scale_rows, idx, 0, S)
+        for quad in range(QUADS):
             nc.sync.dma_start(
-                v_scale[32 * q : 32 * q + 4, :, :].bitcast(I32),
-                picked_scale_rows[12 * q : 12 * q + 12, :].bitcast(I32),
+                v_scale[32 * quad : 32 * quad + ROWS, :, :].bitcast(I32),
+                picked_scale_rows[PASSES * ROWS * quad : PASSES * ROWS * (quad + 1), :].bitcast(I32),
             )
-        tab_tiles.append(load_words(keep.tile([P, T], U32, name="tab_last"), tab_words, 2))
+        tab_tiles.append(load_words("tab_last", tab_words, 2))
         w1_raw.extend(load_w1(a) for a in range(1, PASSES))
-        tab2_tile = load_words(keep.tile([P, T2], U32, name="tab2_tile"), tab2_words, 0)
+        tab2_tile = load_words("tab2_tile", tab2_words, 0)
 
-        for q in range(QUADS):
-            nc.gpsimd.dma_start(
-                tab2_scale_rows[32 * q : 32 * q + 4, :].bitcast(I32),
-                tab2_scales[0, 4 * q : 4 * q + 4, :].bitcast(I32),
-            )
         ident = keep.tile([P, P], F32, name="ident")
         make_identity(nc, ident[:])
         vec_rows = keep.tile([P, P], F32, name="vec_rows")
@@ -133,104 +146,106 @@ def tile_list_swab_mode_scores_kernel(
         nc.gpsimd.dma_start(gain_sb[:], gain.rearrange("(p i) -> p i", i=PACK))
 
         v_codes = [keep.tile([P, S], U32, name="v_codes%d" % a, align_bytes=64) for a in range(PASSES)]
-        b_banks = [bank(jt, [P, BANK]) for jt in range(J_TILES)]
+        v2_scale = keep.tile([P, S2], U8, name="v2_scale", align_bytes=64)
+        gather(v_codes[0], tab_tiles[0], idx, 0, S)
+        gather(v2_scale, tab2_scale_rows, idx2, 0, S2)
+        gather(v_codes[1], tab_tiles[1], idx, 0, S)
+        gather(v_codes[2], tab_tiles[2], idx, 0, S // 2)
+        gather(v_codes[2], tab_tiles[2], idx, S // 2, S)
 
-        def gather_words(dst, table, offsets, lo, hi):
-            nc.vector.tensor_copy(dst[:, lo:hi], table[:].indirect(offsets[:, lo // 16 : hi // 16]))
-
-        def first_product(acc, jt, a, codes, scale):
+        def window_product(acc, jt, a, codes, scale):
             cols = slice(jt * P, (jt + 1) * P)
             nc.tensor.matmul_mx(
                 out=acc[:], lhsT=v_codes[a][:, cols].bitcast(FP8X4), lhsT_scale=v_scale[:, a, cols],
                 rhs=codes, rhs_scale=scale, start=(a == 0), stop=(a == PASSES - 1),
             )
 
-        gather_words(v_codes[0], tab_tiles[0], idx, 0, S)
-        gather_words(v_codes[1], tab_tiles[1], idx, 0, S)
-        v2_scale = staged(0, [P, S2], U8)
-        nc.vector.tensor_copy(v2_scale[:], tab2_scale_rows[:].indirect(idx2[:]))
-        gather_words(v_codes[2], tab_tiles[2], idx, 0, S // 2)
-        gather_words(v_codes[2], tab_tiles[2], idx, S // 2, S)
-
+        background_banks = [bank(jt, [P, BANK]) for jt in range(J_TILES)]
         for a in range(PASSES):
             for jt in range(J_TILES):
-                first_product(b_banks[jt], jt, a, w4_codes[:, a, :].bitcast(FP4X4), w4_scale[:, a, :])
-        b_sb = keep.tile([P, J_TILES, PACK, P], F32, name="b_sb")
+                window_product(background_banks[jt], jt, a, w4_codes[:, a, :].bitcast(FP4X4), w4_scale[:, a, :])
+        background = keep.tile([P, J_TILES, PACK, P], F32, name="background")
         for jt in range(J_TILES):
-            nc.scalar.copy(b_sb[:, jt, :, :], b_banks[jt][:].rearrange("j (p i) -> j i p", i=PACK))
+            nc.scalar.copy(background[:, jt, :, :], background_banks[jt][:].rearrange("j (p i) -> j i p", i=PACK))
 
         for a in range(1, PASSES):
             quantize_w1(a)
 
-        A_BANKS = 5
-        a_banks = {}
-
-        def response(jt, passes):
-            if jt not in a_banks:
-                a_banks[jt] = bank(jt % A_BANKS, [P, BANK])
-            for a in passes:
-                first_product(a_banks[jt], jt, a, w1_codes[:, a, :].bitcast(FP8X4), w1_scale[:, a, :])
-
+        response_banks = {}
+        turned_banks = {}
         h_bf = keep.tile([P, S, PACK], BF16, name="h_bf", align_bytes=64)
         h_codes = keep.tile([P, S], U32, name="h_codes", align_bytes=64)
         h_scale = keep.tile([P, S], U8, name="h_scale", align_bytes=64)
         v2_codes = keep.tile([P, S2], U32, name="v2_codes", align_bytes=64)
-        u_banks = {}
+        scalar_gain_tiles = J_TILES - VECTOR_GAIN_TILES
+        h_rows = keep.tile([P, PACK, scalar_gain_tiles * P], BF16, name="h_rows")
 
-        def capped(jt):
-            u = ring.tile([P, PACK, P], F32, name="u")
+        def response(jt):
+            response_banks[jt] = bank(jt % RESPONSE_BANKS, [P, BANK])
+            for a in range(PASSES):
+                window_product(response_banks[jt], jt, a, w1_codes[:, a, :].bitcast(FP8X4), w1_scale[:, a, :])
+
+        def cap_and_turn(jt):
+            diff = ring.tile([P, PACK, P], F32, name="diff")
             nc.vector.scalar_tensor_tensor(
-                out=u[:], in0=a_banks[jt][:].rearrange("j (p i) -> j i p", i=PACK),
-                scalar=vec_cols[:, 0, jt : jt + 1], in1=b_sb[:, jt, :, :],
+                out=diff[:], in0=response_banks[jt][:].rearrange("j (p i) -> j i p", i=PACK),
+                scalar=vec_cols[:, 0, jt : jt + 1], in1=background[:, jt, :, :],
                 op0=ALU.min, op1=ALU.subtract,
             )
-            u_banks[jt] = bank(A_BANKS + jt % (BANKS - A_BANKS), [P, PACK, P])
+            turned_banks[jt] = bank(RESPONSE_BANKS + jt % (BANKS - RESPONSE_BANKS), [P, PACK, P])
             for i in range(PACK):
-                nc.tensor.transpose(u_banks[jt][:, i, :], u[:, i, :], ident[:])
+                nc.tensor.transpose(turned_banks[jt][:, i, :], diff[:, i, :], ident[:])
 
-        h_planes = keep.tile([P, PACK, S], BF16, name="h_planes")
-
-        def gained(jt):
-            for i in range(PACK):
-                nc.scalar.activation(
-                    h_planes[:, i, jt * P : (jt + 1) * P], u_banks[jt][:, i, :], ACT.Copy,
-                    scale=gain_sb[:, i : i + 1],
+        def apply_gain(jt):
+            cols = slice(jt * P, (jt + 1) * P)
+            if jt < scalar_gain_tiles:
+                for i in range(PACK):
+                    nc.scalar.activation(
+                        h_rows[:, i, cols], turned_banks[jt][:, i, :], ACT.Copy, scale=gain_sb[:, i : i + 1]
+                    )
+            else:
+                nc.vector.tensor_tensor(
+                    out=h_bf[:, cols, :], in0=turned_banks[jt][:].rearrange("p i j -> p j i"),
+                    in1=gain_sb[:].unsqueeze(1).to_broadcast([P, P, PACK]), op=ALU.mult,
                 )
 
-        def quantize_h(lo, hi):
-            nc.vector.tensor_copy(
-                h_bf[:, lo:hi, :].rearrange("p (c n) i -> p c i n", n=4),
-                h_planes[:, :, lo:hi].rearrange("p i (c n) -> p c i n", n=4),
-            )
-            nc.vector.quantize_mx(
-                out=h_codes[:, lo:hi].bitcast(FP8X4), scales=h_scale[:, lo:hi],
-                in_=h_bf[:, lo:hi, :].rearrange("p j i -> p (j i)"),
-            )
+        def quantize_h(first_jt):
+            cols = slice(first_jt * P, (first_jt + 2) * P)
+            if first_jt < scalar_gain_tiles:
+                interleave(h_bf[:, cols, :], h_rows[:, :, cols])
+            quantize(h_codes[:, cols], h_scale[:, cols], h_bf[:, cols, :])
 
-        for jt in range(A_BANKS):
-            response(jt, range(PASSES))
+        for jt in range(RESPONSE_BANKS):
+            response(jt)
         for jt in range(J_TILES):
-            capped(jt)
-            if jt + A_BANKS < J_TILES:
-                response(jt + A_BANKS, range(PASSES))
-            gained(jt)
+            cap_and_turn(jt)
+            if jt + RESPONSE_BANKS < J_TILES:
+                response(jt + RESPONSE_BANKS)
             if jt >= 3 and jt % 2 == 1:
-                quantize_h((jt - 3) * P, (jt - 1) * P)
-        gather_words(v2_codes, tab2_tile, idx2, 0, 256)
-        quantize_h(S - 2 * P, S)
-        gather_words(v2_codes, tab2_tile, idx2, 256, S2)
+                quantize_h(jt - 3)
+            apply_gain(jt)
+        gather(v2_codes, tab2_tile, idx2, 0, FIRST_COMPOUNDS)
+        quantize_h(J_TILES - 2)
+        gather(v2_codes, tab2_tile, idx2, FIRST_COMPOUNDS, S2)
 
-        for mt in range(M_TILES):
+        e_tiles = {}
+
+        def scores(mt):
             rows = slice(mt * P, (mt + 1) * P)
-            e_sb = ring.tile([P, S], F32, name="e_sb")
-            for half in range(2):
+            e_tiles[mt] = ring.tile([P, S], F32, name="e_sb")
+            for half in range(S // BANK):
                 cols = slice(half * BANK, (half + 1) * BANK)
-                e_bank = bank((3 + (2 * mt + half) % 4) % A_BANKS, [P, BANK])
+                e_bank = bank(SCORE_BANKS[(2 * mt + half) % len(SCORE_BANKS)], [P, BANK])
                 nc.tensor.matmul_mx(
                     out=e_bank[:], lhsT=v2_codes[:, rows].bitcast(FP8X4), lhsT_scale=v2_scale[:, rows],
                     rhs=h_codes[:, cols].bitcast(FP8X4), rhs_scale=h_scale[:, cols], start=True, stop=True,
                 )
-                nc.scalar.copy(e_sb[:, cols], e_bank[:])
+                nc.scalar.copy(e_tiles[mt][:, cols], e_bank[:])
+
+        scores(0)
+        scores(1)
+        for mt in range(M_TILES):
+            rows = slice(mt * P, (mt + 1) * P)
             picked = ring.tile([P, 2, NPAIR], F32, name="picked")
             sig = ring.tile([P, 2, NPAIR], F32, name="sig")
             res = ring.tile([P, NPAIR], F32, name="res")
@@ -238,10 +253,12 @@ def tile_list_swab_mode_scores_kernel(
             for lo in range(0, NPAIR, width):
                 pairs = slice(lo, lo + width)
                 for mode, pos in enumerate((p1, p2)):
-                    nc.vector.tensor_copy(
-                        picked[:, mode, pairs], e_sb[:].indirect(pos[:, lo // 16 : (lo + width) // 16])
-                    )
+                    gather(picked[:, mode, :], e_tiles[mt], pos, lo, lo + width)
                     nc.scalar.activation(sig[:, mode, pairs], picked[:, mode, pairs], ACT.Sigmoid)
+            if mt + 2 < M_TILES:
+                scores(mt + 2)
+            for lo in range(0, NPAIR, width):
+                pairs = slice(lo, lo + width)
                 nc.vector.scalar_tensor_tensor(
                     out=res[:, pairs], in0=sig[:, 0, pairs], scalar=vec_cols[:, 1, mt : mt + 1],
                     in1=sig[:, 1, pairs], op0=ALU.mult, op1=ALU.mult,

from contextlib import ExitStack

import concourse.mybir as mybir
from concourse.masks import make_identity

K, T, S, H, T2, S2, NPAIR = 1536, 4096, 1024, 512, 2048, 1024, 512
FLOPS = 2 * (2 * K * H * S) + 2 * H * S2 * S

F32 = mybir.dt.float32
BF16 = mybir.dt.bfloat16
I32 = mybir.dt.int32
U32 = mybir.dt.uint32
U16 = mybir.dt.uint16
U8 = mybir.dt.uint8
FP8X4 = mybir.dt.float8_e4m3fn_x4
FP4X4 = mybir.dt.float4_e2m1fn_x4
ALU = mybir.AluOpType
ACT = mybir.ActivationFunctionType

P = 128
PACK = 4
PASSES = K // (P * PACK)
BLOCKS = 16
QUADS = 4
ROWS = BLOCKS // QUADS
STRIPE = 16
J_TILES = S // P
M_TILES = S2 // P
BANK = 512
BANKS = 8
RESPONSE_BANKS = 5
SCORE_BANKS = (3, 4, 0, 1)
VECTOR_GAIN_TILES = 2
FIRST_COMPOUNDS = 2 * P


def tile_list_swab_mode_scores_kernel(
    tc, tab_words, tab_scales, offs, w1, w4_words, w4_scales, cap, gain,
    tab2_words, tab2_scales, offs2, danger, pos1, pos2, out,
):
    nc = tc.nc
    with ExitStack() as ctx:
        keep = ctx.enter_context(tc.tile_pool(name="keep", bufs=1))
        ring = ctx.enter_context(tc.tile_pool(name="ring", bufs=3))
        psum = ctx.enter_context(tc.psum_pool(name="psum", bufs=1))

        def bank(b, shape):
            return psum.tile(shape, F32, name="bank%d" % b, tag="bank%d" % b)

        def zeroed(name, shape):
            tile = keep.tile(shape, U8, name=name, align_bytes=64)
            flat = tile[:] if len(shape) == 2 else tile[:].rearrange("p a c -> p (a c)")
            nc.vector.memset(flat.bitcast(I32), 0)
            return tile

        def load_words(name, table, a):
            tile = keep.tile([P, table.shape[2]], U32, name=name)
            nc.sync.dma_start(tile[:].bitcast(I32), table[a].rearrange("p n i -> p (n i)").bitcast(I32))
            return tile

        def load_w1(a):
            raw = keep.tile([P, PACK, H], F32, name="w1_raw%d" % a)
            rows = w1[a * P * PACK : (a + 1) * P * PACK, :]
            nc.sync.dma_start(raw[:], rows.rearrange("(p i) r -> p i r", i=PACK))
            return raw

        def gather(dst, window, offsets, lo, hi):
            nc.vector.tensor_copy(dst[:, lo:hi], window[:].indirect(offsets[:, lo // STRIPE : hi // STRIPE]))

        def interleave(dst, src):
            nc.vector.tensor_copy(
                dst.rearrange("p (c n) i -> p c i n", n=4), src.rearrange("p i (c n) -> p c i n", n=4)
            )

        def quantize(codes, scale, grouped):
            nc.vector.quantize_mx(
                out=codes.bitcast(FP8X4), scales=scale, in_=grouped.rearrange("p c i -> p (c i)")
            )

        idx = keep.tile([P, S // STRIPE], U16, name="idx")
        idx2 = keep.tile([P, S2 // STRIPE], U16, name="idx2")
        p1 = keep.tile([P, NPAIR // STRIPE], U16, name="p1")
        p2 = keep.tile([P, NPAIR // STRIPE], U16, name="p2")
        nc.sync.dma_start(idx[:], offs)
        nc.sync.dma_start(idx2[:], offs2)
        nc.sync.dma_start(p1[:], pos1)
        nc.sync.dma_start(p2[:], pos2)

        tab_scale_rows = zeroed("tab_scale_rows", [P, T])
        tab2_scale_rows = zeroed("tab2_scale_rows", [P, T2])
        w4_scale = zeroed("w4_scale", [P, PASSES, H])
        v_scale = zeroed("v_scale", [P, PASSES, S])

        w1_raw = [load_w1(0)]
        nc.sync.dma_start(
            tab_scale_rows[0 : BLOCKS * PASSES, :].bitcast(I32),
            tab_scales.rearrange("a q t -> q a t").bitcast(I32),
        )
        w4_codes = keep.tile([P, PASSES, 2 * H], U8, name="w4_codes", align_bytes=64)
        nc.sync.dma_start(w4_codes[:].bitcast(I32), w4_words.rearrange("a p c -> p a c").bitcast(I32))
        for quad in range(QUADS):
            nc.sync.dma_start(
                tab2_scale_rows[32 * quad : 32 * quad + ROWS, :].bitcast(I32),
                tab2_scales[0, ROWS * quad : ROWS * (quad + 1), :].bitcast(I32),
            )
        tab_tiles = [load_words("tab_first", tab_words, 0)]
        for quad in range(QUADS):
            nc.sync.dma_start(
                w4_scale[32 * quad : 32 * quad + ROWS, :, :].bitcast(I32),
                w4_scales[:, ROWS * quad : ROWS * (quad + 1), :].rearrange("a q r -> q a r").bitcast(I32),
            )
        tab_tiles.append(load_words("tab_mid", tab_words, 1))

        w1_codes = keep.tile([P, PASSES, H], U32, name="w1_codes", align_bytes=64)
        w1_scale = keep.tile([P, PASSES, H], U8, name="w1_scale", align_bytes=64)

        def quantize_w1(a):
            w1_bf = ring.tile([P, H, PACK], BF16, name="w1_bf", align_bytes=64)
            interleave(w1_bf[:], w1_raw[a][:])
            quantize(w1_codes[:, a, :], w1_scale[:, a, :], w1_bf[:])

        quantize_w1(0)

        picked_scale_rows = keep.tile([P, S], U8, name="picked_scale_rows")
        gather(picked_scale_rows, tab_scale_rows, idx, 0, S)
        for quad in range(QUADS):
            nc.sync.dma_start(
                v_scale[32 * quad : 32 * quad + ROWS, :, :].bitcast(I32),
                picked_scale_rows[PASSES * ROWS * quad : PASSES * ROWS * (quad + 1), :].bitcast(I32),
            )
        tab_tiles.append(load_words("tab_last", tab_words, 2))
        w1_raw.extend(load_w1(a) for a in range(1, PASSES))
        tab2_tile = load_words("tab2_tile", tab2_words, 0)

        ident = keep.tile([P, P], F32, name="ident")
        make_identity(nc, ident[:])
        vec_rows = keep.tile([P, P], F32, name="vec_rows")
        nc.gpsimd.memset(vec_rows[:], 0.0)
        for n, vec in enumerate((cap, danger)):
            nc.gpsimd.dma_start(vec_rows[n * J_TILES : (n + 1) * J_TILES, :], vec.rearrange("(t p) -> t p", p=P))
        vec_bank = bank(BANKS - 1, [P, P])
        nc.tensor.transpose(vec_bank[:], vec_rows[:], ident[:])
        vec_cols = keep.tile([P, 2, J_TILES], F32, name="vec_cols")
        nc.scalar.copy(vec_cols[:].rearrange("p n t -> p (n t)"), vec_bank[:, 0 : 2 * J_TILES])
        gain_sb = keep.tile([P, PACK], F32, name="gain_sb")
        nc.gpsimd.dma_start(gain_sb[:], gain.rearrange("(p i) -> p i", i=PACK))

        v_codes = [keep.tile([P, S], U32, name="v_codes%d" % a, align_bytes=64) for a in range(PASSES)]
        v2_scale = keep.tile([P, S2], U8, name="v2_scale", align_bytes=64)
        gather(v_codes[0], tab_tiles[0], idx, 0, S)
        gather(v2_scale, tab2_scale_rows, idx2, 0, S2)
        gather(v_codes[1], tab_tiles[1], idx, 0, S)
        gather(v_codes[2], tab_tiles[2], idx, 0, S // 2)
        gather(v_codes[2], tab_tiles[2], idx, S // 2, S)

        def window_product(acc, jt, a, codes, scale):
            cols = slice(jt * P, (jt + 1) * P)
            nc.tensor.matmul_mx(
                out=acc[:], lhsT=v_codes[a][:, cols].bitcast(FP8X4), lhsT_scale=v_scale[:, a, cols],
                rhs=codes, rhs_scale=scale, start=(a == 0), stop=(a == PASSES - 1),
            )

        background_banks = [bank(jt, [P, BANK]) for jt in range(J_TILES)]
        for a in range(PASSES):
            for jt in range(J_TILES):
                window_product(background_banks[jt], jt, a, w4_codes[:, a, :].bitcast(FP4X4), w4_scale[:, a, :])
        background = keep.tile([P, J_TILES, PACK, P], F32, name="background")
        for jt in range(J_TILES):
            nc.scalar.copy(background[:, jt, :, :], background_banks[jt][:].rearrange("j (p i) -> j i p", i=PACK))

        for a in range(1, PASSES):
            quantize_w1(a)

        response_banks = {}
        turned_banks = {}
        h_bf = keep.tile([P, S, PACK], BF16, name="h_bf", align_bytes=64)
        h_codes = keep.tile([P, S], U32, name="h_codes", align_bytes=64)
        h_scale = keep.tile([P, S], U8, name="h_scale", align_bytes=64)
        v2_codes = keep.tile([P, S2], U32, name="v2_codes", align_bytes=64)
        scalar_gain_tiles = J_TILES - VECTOR_GAIN_TILES
        h_rows = keep.tile([P, PACK, scalar_gain_tiles * P], BF16, name="h_rows")

        def response(jt):
            response_banks[jt] = bank(jt % RESPONSE_BANKS, [P, BANK])
            for a in range(PASSES):
                window_product(response_banks[jt], jt, a, w1_codes[:, a, :].bitcast(FP8X4), w1_scale[:, a, :])

        def cap_and_turn(jt):
            diff = ring.tile([P, PACK, P], F32, name="diff")
            nc.vector.scalar_tensor_tensor(
                out=diff[:], in0=response_banks[jt][:].rearrange("j (p i) -> j i p", i=PACK),
                scalar=vec_cols[:, 0, jt : jt + 1], in1=background[:, jt, :, :],
                op0=ALU.min, op1=ALU.subtract,
            )
            turned_banks[jt] = bank(RESPONSE_BANKS + jt % (BANKS - RESPONSE_BANKS), [P, PACK, P])
            for i in range(PACK):
                nc.tensor.transpose(turned_banks[jt][:, i, :], diff[:, i, :], ident[:])

        def apply_gain(jt):
            cols = slice(jt * P, (jt + 1) * P)
            if jt < scalar_gain_tiles:
                for i in range(PACK):
                    nc.scalar.activation(
                        h_rows[:, i, cols], turned_banks[jt][:, i, :], ACT.Copy, scale=gain_sb[:, i : i + 1]
                    )
            else:
                nc.vector.tensor_tensor(
                    out=h_bf[:, cols, :], in0=turned_banks[jt][:].rearrange("p i j -> p j i"),
                    in1=gain_sb[:].unsqueeze(1).to_broadcast([P, P, PACK]), op=ALU.mult,
                )

        def quantize_h(first_jt):
            cols = slice(first_jt * P, (first_jt + 2) * P)
            if first_jt < scalar_gain_tiles:
                interleave(h_bf[:, cols, :], h_rows[:, :, cols])
            quantize(h_codes[:, cols], h_scale[:, cols], h_bf[:, cols, :])

        for jt in range(RESPONSE_BANKS):
            response(jt)
        for jt in range(J_TILES):
            cap_and_turn(jt)
            if jt + RESPONSE_BANKS < J_TILES:
                response(jt + RESPONSE_BANKS)
            if jt >= 3 and jt % 2 == 1:
                quantize_h(jt - 3)
            apply_gain(jt)
        gather(v2_codes, tab2_tile, idx2, 0, FIRST_COMPOUNDS)
        quantize_h(J_TILES - 2)
        gather(v2_codes, tab2_tile, idx2, FIRST_COMPOUNDS, S2)

        e_tiles = {}

        def scores(mt):
            rows = slice(mt * P, (mt + 1) * P)
            e_tiles[mt] = ring.tile([P, S], F32, name="e_sb")
            for half in range(S // BANK):
                cols = slice(half * BANK, (half + 1) * BANK)
                e_bank = bank(SCORE_BANKS[(2 * mt + half) % len(SCORE_BANKS)], [P, BANK])
                nc.tensor.matmul_mx(
                    out=e_bank[:], lhsT=v2_codes[:, rows].bitcast(FP8X4), lhsT_scale=v2_scale[:, rows],
                    rhs=h_codes[:, cols].bitcast(FP8X4), rhs_scale=h_scale[:, cols], start=True, stop=True,
                )
                nc.scalar.copy(e_tiles[mt][:, cols], e_bank[:])

        scores(0)
        scores(1)
        for mt in range(M_TILES):
            rows = slice(mt * P, (mt + 1) * P)
            picked = ring.tile([P, 2, NPAIR], F32, name="picked")
            sig = ring.tile([P, 2, NPAIR], F32, name="sig")
            res = ring.tile([P, NPAIR], F32, name="res")
            width = NPAIR // 2 if mt == M_TILES - 1 else NPAIR
            for lo in range(0, NPAIR, width):
                pairs = slice(lo, lo + width)
                for mode, pos in enumerate((p1, p2)):
                    gather(picked[:, mode, :], e_tiles[mt], pos, lo, lo + width)
                    nc.scalar.activation(sig[:, mode, pairs], picked[:, mode, pairs], ACT.Sigmoid)
            if mt + 2 < M_TILES:
                scores(mt + 2)
            for lo in range(0, NPAIR, width):
                pairs = slice(lo, lo + width)
                nc.vector.scalar_tensor_tensor(
                    out=res[:, pairs], in0=sig[:, 0, pairs], scalar=vec_cols[:, 1, mt : mt + 1],
                    in1=sig[:, 1, pairs], op0=ALU.mult, op1=ALU.mult,
                )
                nc.sync.dma_start(out[rows, pairs], res[:, pairs])
